import numpy as np
import ml_dtypes


def mxq(x, axis, fmt="e4m3"):
    dtype, down = {"e4m3": (ml_dtypes.float8_e4m3fn, 7), "e5m2": (ml_dtypes.float8_e5m2, 14)}[fmt]
    v = np.moveaxis(np.asarray(x, np.float32).astype(ml_dtypes.bfloat16).astype(np.float64), axis, -1)
    blocks = v.reshape(v.shape[:-1] + (-1, 32))
    amax = np.abs(blocks).max(-1, keepdims=True)
    byte = np.maximum(np.where(amax > 0, np.frexp(amax)[1] - 1 + 127, 0) - down, 1)
    scale = np.exp2(byte - 127.0)
    codes = (blocks / scale).astype(np.float32).astype(dtype).astype(np.float64)
    return np.moveaxis((codes * scale).reshape(v.shape), -1, axis)


WIDE = False


def mx_kscale(k):
    if not WIDE:
        return np.ones(k)
    levels = np.array([10, -10, 5, -5, 0])
    if k % 512:
        return np.exp2(np.random.permutation(np.resize(levels, k // 32))).repeat(32)
    a = np.empty((k // 512, 16))
    for p in range(k // 512):
        a[p, :8] = np.random.permutation(np.resize(levels, 8))
        for g in range(8):
            far = levels[np.abs(levels - a[p, g]) >= 10]
            a[p, g + 8] = far[np.random.randint(len(far))]
    return np.exp2(a.ravel()).repeat(32)


def f64(x):
    return np.asarray(x).astype(np.float64)


def striped(idx):
    return np.tile(idx.reshape(-1, 16).T, (8, 1)).astype(np.uint16)


def unstriped(offs):
    return offs[:16].T.reshape(-1).astype(np.int64)


E2M1 = np.array([0.0, 0.5, 1.0, 1.5, 2.0, 3.0, 4.0, 6.0, -0.0, -0.5, -1.0, -1.5, -2.0, -3.0, -4.0, -6.0])


def pack_weight(w, fmt):
    k, n = w.shape
    w = f64(np.asarray(w, np.float32).astype(ml_dtypes.bfloat16)).reshape(k // 32, 32, n)
    amax = np.abs(w).max(1)
    if fmt == "e4m3":
        byte = np.frexp(amax)[1] - 1 + 127 - 7
    else:
        mant, ex = np.frexp(amax / 6.0)
        byte = np.where(mant > 0.5, ex, ex - 1) + 127
    byte = np.clip(np.where(amax > 0, byte, 1), 1, 254)
    scaled = (w * np.exp2(127.0 - byte)[:, None, :]).reshape(k, n).astype(np.float32)
    by_word = np.ascontiguousarray(scaled.reshape(k // 512, 128, 4, n).transpose(0, 1, 3, 2))
    if fmt == "e4m3":
        words = by_word.astype(ml_dtypes.float8_e4m3fn).view(np.uint8)
    else:
        c = by_word.astype(ml_dtypes.float4_e2m1fn).view(np.uint8) & 0xF
        words = (c[..., 0::2] | (c[..., 1::2] << 4)).reshape(k // 512, 128, 2 * n)
    return np.ascontiguousarray(words), np.ascontiguousarray(byte.astype(np.uint8).reshape(k // 512, 16, n))


def unpack_weight(words, scales, fmt):
    g, _, n = scales.shape
    words = np.ascontiguousarray(words).reshape(g, 128, n, -1)
    if fmt == "e4m3":
        vals = words.view(ml_dtypes.float8_e4m3fn).astype(np.float64)
    else:
        nib = np.empty((g, 128, n, 4), np.uint8)
        nib[..., 0::2] = words & 0xF
        nib[..., 1::2] = words >> 4
        vals = E2M1[nib]
    vals = vals * np.repeat(np.exp2(scales.astype(np.float64) - 127.0), 8, axis=1)[..., None]
    return vals.transpose(0, 1, 3, 2).reshape(g * 512, n)


def gelu(v):
    return 0.5 * v * (1.0 + np.tanh(np.sqrt(2.0 / np.pi) * (v + 0.044715 * v**3)))


def bf(x):
    return np.asarray(x, np.float32).astype(ml_dtypes.bfloat16)


def planes(Y):
    n, m = Y.shape
    b = f64(bf(Y)).reshape(n // 32, 32, m)
    amax = np.abs(b).max(1)
    byte = np.clip(np.where(amax > 0, np.frexp(amax)[1] - 1 + 127 - 7, 1), 1, 254)
    codes = (b * np.exp2(127.0 - byte)[:, None, :]).reshape(n, m).astype(np.float32).astype(ml_dtypes.float8_e4m3fn).view(np.uint8)
    words = codes.reshape(n // 512, 128, 4, m).transpose(0, 1, 3, 2)
    return np.ascontiguousarray(words), np.ascontiguousarray(byte.astype(np.uint8).reshape(n // 512, 16, m))


K, H, N, T, S, P = 1024, 1024, 512, 4096, 1024, 512

def setup_inputs():
    n = np.random.standard_normal
    s = mx_kscale(K)[:, None]
    u = mx_kscale(H)[:, None]
    tab_words, tab_scales = pack_weight(n((K, T)) * s, "e4m3")
    wa = 1.3 * n((H, N)) / np.sqrt(H) / u * np.exp(0.8 * n(N))
    wa_words, wa_scales = pack_weight(wa, "e2m1")
    return {
        "tab_words": tab_words,
        "tab_scales": tab_scales,
        "offs": striped(np.random.permutation(T)[:S]),
        "pos1": striped(np.random.permutation(S)[:P]),
        "pos2": striped(np.random.permutation(S)[:P]),
        "w1": (1.3 * n((K, H)) / np.sqrt(K) / s).astype(np.float32),
        "b1": (0.7 * n(H)).astype(np.float32),
        "gain": (np.exp(0.3 * n(H)) * u[:, 0]).astype(np.float32),
        "va": (1.0 + 0.5 * n(H)).astype(np.float32),
        "cb": ((0.4 * n(H) - 0.2) * u[:, 0]).astype(np.float32),
        "wa_words": wa_words,
        "wa_scales": wa_scales,
        "wb": (1.3 * n((H, N)) / np.sqrt(H) / u).astype(np.float32),
    }

def reference(tab_words, tab_scales, offs, pos1, pos2, w1, b1, gain, va, cb, wa_words, wa_scales, wb):
    v = unpack_weight(tab_words, tab_scales, "e4m3")[:, unstriped(offs)]
    d = mxq(f64(w1), 0, "e4m3").T @ v
    h = np.tanh(d + f64(b1)[:, None]) * f64(gain)[:, None]
    xa = h[:, unstriped(pos1)] * f64(va)[:, None]
    xb = np.maximum(h[:, unstriped(pos2)], f64(cb)[:, None])
    ya = unpack_weight(wa_words, wa_scales, "e2m1").T @ mxq(xa, 0, "e4m3")
    yb = mxq(f64(wb), 0, "e4m3").T @ mxq(xb, 0, "e4m3")
    y = ya * yb
    words, scales = planes(y)
    return y, words, scales

@@ -1,0 +1,307 @@
+from contextlib import ExitStack
+
+import concourse.mybir as mybir
+
+K, H, N, T, S, NPAIR = 1024, 1024, 512, 4096, 1024, 512
+FLOPS = 2 * K * H * S + 2 * 2 * H * N * NPAIR
+
+F32 = mybir.dt.float32
+BF16 = mybir.dt.bfloat16
+I32 = mybir.dt.int32
+U32 = mybir.dt.uint32
+U16 = mybir.dt.uint16
+U8 = mybir.dt.uint8
+FP8X4 = mybir.dt.float8_e4m3fn_x4
+FP4X4 = mybir.dt.float4_e2m1fn_x4
+MULT = mybir.AluOpType.mult
+MAX = mybir.AluOpType.max
+TANH = mybir.ActivationFunctionType.Tanh
+
+P = 128
+PACK = 4
+KP = P * PACK
+BANK = 512
+PIECES = ((0, 256), (256, 512))
+HEAD_SPLIT = 84
+
+
+def tile_list_rop_vessel_ridge_kernel(
+    tc, tab_words, tab_scales, offs, pos1, pos2, w1, b1, gain, va, cb, wa_words, wa_scales, wb, out_0, out_1, out_2
+):
+    nc = tc.nc
+    with ExitStack() as ctx:
+        lists = ctx.enter_context(tc.tile_pool(name="lists", bufs=1))
+        keep = ctx.enter_context(tc.tile_pool(name="keep", bufs=1))
+        ring = ctx.enter_context(tc.tile_pool(name="ring", bufs=4))
+        psum = ctx.enter_context(tc.psum_pool(name="psum", bufs=8))
+
+        def kept(shape, dtype, name):
+            return keep.tile(shape, dtype, name=name, align_bytes=64)
+
+        def staged(width, name):
+            return ring.tile([P, width], BF16, name=name, tag="staged", align_bytes=64)
+
+        def copy_on(engine, out, in_):
+            if engine == "vector":
+                nc.vector.tensor_copy(out=out, in_=in_)
+            else:
+                nc.scalar.copy(out=out, in_=in_)
+
+        offs_t = lists.tile([P, S // 16], U16, name="offs_t")
+        pos1_t = lists.tile([P, NPAIR // 16], U16, name="pos1_t")
+        pos2_t = lists.tile([P, NPAIR // 16], U16, name="pos2_t")
+        nc.sync.dma_start(offs_t[:], offs)
+
+        scale_window = kept([P, T], U8, "scale_window")
+        nc.vector.memset(scale_window[:].bitcast(I32), 0)
+        nc.gpsimd.dma_start(
+            out=scale_window[0:P:4, :].bitcast(I32),
+            in_=tab_scales.rearrange("a q t -> (a q) t").bitcast(I32),
+        )
+
+        table = [kept([P, T], U32, f"table{a}") for a in range(2)]
+        nc.sync.dma_start(out=table[0][:].bitcast(I32), in_=tab_words[0].rearrange("p t i -> p (t i)").bitcast(I32))
+        wa_raw = kept([P, 2, 2 * N], U8, "wa_raw")
+        nc.sync.dma_start(out=wa_raw[:].bitcast(I32), in_=wa_words.rearrange("a p c -> p a c").bitcast(I32))
+        nc.sync.dma_start(out=table[1][:].bitcast(I32), in_=tab_words[1].rearrange("p t i -> p (t i)").bitcast(I32))
+
+        def load_weight(w, a, b):
+            raw = ring.tile([P, PACK, KP], F32, name="raw", tag="raw")
+            nc.sync.dma_start(
+                out=raw[:], in_=w[a * KP : (a + 1) * KP, b * KP : (b + 1) * KP].rearrange("(p j) c -> p j c", j=PACK)
+            )
+            return raw
+
+        w1_raw = {}
+        w1_raw[0, 0] = load_weight(w1, 0, 0)
+        w1_raw[1, 0] = load_weight(w1, 1, 0)
+        nc.sync.dma_start(pos1_t[:], pos1)
+        nc.sync.dma_start(pos2_t[:], pos2)
+        w1_raw[0, 1] = load_weight(w1, 0, 1)
+        w1_raw[1, 1] = load_weight(w1, 1, 1)
+
+        def load_vector(v, name):
+            t = kept([P, 2, PACK], F32, name)
+            nc.scalar.dma_start(out=t[:], in_=v.rearrange("(b p t) -> p b t", b=2, t=PACK))
+            return t
+
+        gain_t = load_vector(gain, "gain_t")
+        va_t = load_vector(va, "va_t")
+        b1_t = load_vector(b1, "b1_t")
+        cb_t = load_vector(cb, "cb_t")
+
+        was_raw = kept([P, 2, N], U8, "was_raw")
+        nc.vector.memset(was_raw[:].bitcast(I32), 0)
+        for q in range(4):
+            nc.scalar.dma_start(
+                out=was_raw[32 * q : 32 * q + 4, :, :].bitcast(I32),
+                in_=wa_scales[:, 4 * q : 4 * q + 4, :].rearrange("a r c -> r a c").bitcast(I32),
+            )
+
+        picked_scales = kept([P, S], U8, "picked_scales")
+        nc.vector.tensor_copy(out=picked_scales[:], in_=scale_window[:].indirect(offs_t[:]))
+        v_scales = kept([P, 2, S], U8, "v_scales")
+        nc.vector.memset(v_scales[:].bitcast(I32), 0)
+        for a in range(2):
+            for q in range(4):
+                first = 64 * a + 16 * q
+                nc.gpsimd.dma_start(
+                    out=v_scales[32 * q : 32 * q + 4, a, :].bitcast(I32),
+                    in_=picked_scales[first : first + 16 : 4, :].bitcast(I32),
+                )
+
+        gain_va = kept([P, 2, PACK], F32, "gain_va")
+        nc.vector.tensor_tensor(out=gain_va[:], in0=gain_t[:], in1=va_t[:], op=MULT)
+        spread = kept([P, 2, PACK, NPAIR], F32, "spread")
+        for b in range(2):
+            for t in range(PACK):
+                nc.scalar.copy(out=spread[:, b, t, :], in_=gain_va[:, b, t : t + 1].to_broadcast([P, NPAIR]))
+
+        v_codes = [kept([P, S], U32, f"v_codes{a}") for a in range(2)]
+        nc.vector.tensor_copy(out=v_codes[0][:], in_=table[0][:].indirect(offs_t[:]))
+
+        wa_codes = kept([P, 2, 2 * N], U8, "wa_codes")
+        nc.vector.tensor_copy(
+            out=wa_codes[:].rearrange("p a (t m e) -> p a m t e", t=PACK, e=2),
+            in_=wa_raw[:].rearrange("p a (m t e) -> p a m t e", t=PACK, e=2),
+        )
+        wa_sc = kept([P, 2, N], U8, "wa_sc")
+        nc.vector.tensor_copy(
+            out=wa_sc[:].rearrange("p a (t m) -> p a m t", t=PACK),
+            in_=was_raw[:].rearrange("p a (m t) -> p a m t", t=PACK),
+        )
+        nc.vector.tensor_copy(out=v_codes[1][:], in_=table[1][:].indirect(offs_t[:]))
+
+        def round_weight(raw, shares, name):
+            rounded = staged(PACK * KP, name)
+            dst = rounded[:].rearrange("p (t m j) -> p m j t", t=PACK, j=PACK)
+            src = raw[:].rearrange("p j (m t) -> p m j t", t=PACK)
+            for engine, m0, m1 in shares:
+                copy_on(engine, dst[:, m0:m1], src[:, m0:m1])
+            return rounded
+
+        def quantize(rounded, name, parts=1):
+            width = rounded.shape[1] // PACK
+            codes = kept([P, width], U32, name + "_codes")
+            scales = kept([P, width], U8, name + "_scales")
+            step = width // parts
+            for c in range(0, width, step):
+                nc.vector.quantize_mx(
+                    out=codes[:, c : c + step].bitcast(FP8X4),
+                    scales=scales[:, c : c + step],
+                    in_=rounded[:, PACK * c : PACK * (c + step)],
+                )
+            return codes, scales
+
+        both = (("vector", 0, HEAD_SPLIT), ("scalar", HEAD_SPLIT, P))
+        w1_q = {}
+        for a in range(2):
+            w1_q[a, 0] = quantize(round_weight(w1_raw[a, 0], both, "w1_bf"), f"w1_{a}0", parts=1 + a)
+
+        wb_raw = [load_weight(wb, a, 0) for a in range(2)]
+
+        def first_stage(b, t):
+            h = ring.tile([P, S], F32, name="h", tag="h", bufs=8)
+            cols = slice(t * P, (t + 1) * P)
+            for half in range(S // BANK):
+                picks = slice(half * BANK, (half + 1) * BANK)
+                bank = psum.tile([P, BANK], F32, name="bank", tag="bank")
+                for a in range(2):
+                    nc.tensor.matmul_mx(
+                        out=bank[:],
+                        lhsT=w1_q[a, b][0][:, cols].bitcast(FP8X4),
+                        lhsT_scale=w1_q[a, b][1][:, cols],
+                        rhs=v_codes[a][:, picks].bitcast(FP8X4),
+                        rhs_scale=v_scales[:, a, picks],
+                        start=(a == 0),
+                        stop=(a == 1),
+                    )
+                nc.scalar.activation(out=h[:, picks], in_=bank[:], func=TANH, bias=b1_t[:, b, t : t + 1])
+            return h
+
+        def pick_vessel(dst, h, b, t):
+            nc.vector.tensor_tensor(out=dst[:, t, :], in0=h[:].indirect(pos1_t[:]), in1=spread[:, b, t, :], op=MULT)
+
+        def pick_ridge(dst, h, t, c0, c1):
+            nc.vector.tensor_copy(out=dst[:, t, :], in_=h[:].indirect(pos2_t[:, c0 // 16 : c1 // 16]))
+
+        def bound_ridge(dst, src, b, t):
+            nc.vector.tensor_scalar(
+                out=dst[:, t, :],
+                in0=src[:, t, :],
+                scalar1=gain_t[:, b, t : t + 1],
+                scalar2=cb_t[:, b, t : t + 1],
+                op0=MULT,
+                op1=MAX,
+            )
+
+        def interleave(src, engine, name):
+            woven = staged(PACK * src.shape[2], name)
+            copy_on(
+                engine,
+                woven[:].rearrange("p (c i t) -> p c t i", i=4, t=PACK),
+                src[:].rearrange("p t (c i) -> p c t i", i=4),
+            )
+            return woven
+
+        h0 = [first_stage(0, t) for t in range(PACK)]
+        w1_bf = [round_weight(w1_raw[a, 1], (("scalar", 0, P),), "w1_bf") for a in range(2)]
+
+        vessel0 = kept([P, PACK, NPAIR], F32, "vessel0")
+        ridge0 = kept([P, PACK, NPAIR], F32, "ridge0")
+        ridge0_bf = kept([P, PACK, NPAIR], BF16, "ridge0_bf")
+        for t in range(PACK):
+            pick_vessel(vessel0, h0[t], 0, t)
+            if t > 0:
+                bound_ridge(ridge0_bf, ridge0, 0, t - 1)
+            if t >= 2:
+                w1_q[t - 2, 1] = quantize(w1_bf[t - 2], f"w1_{t - 2}1")
+            pick_ridge(ridge0, h0[t], t, 0, NPAIR)
+        h1 = [first_stage(1, t) for t in range(PACK)]
+        wb_bf0 = round_weight(wb_raw[0], (("vector", 0, P),), "wb_bf")
+        bound_ridge(ridge0_bf, ridge0, 0, PACK - 1)
+        xa_bf0 = interleave(vessel0, "scalar", "xa_bf")
+        xb_bf0 = interleave(ridge0_bf, "scalar", "xb_bf")
+
+        vessel1 = kept([P, PACK, NPAIR], F32, "vessel1")
+        pick_vessel(vessel1, h1[0], 1, 0)
+        wb_q = [quantize(wb_bf0, "wb0")]
+        pick_vessel(vessel1, h1[1], 1, 1)
+        wb_bf1 = round_weight(wb_raw[1], (("vector", 0, P),), "wb_bf")
+        pick_vessel(vessel1, h1[2], 1, 2)
+        wb_q.append(quantize(wb_bf1, "wb1"))
+        pick_vessel(vessel1, h1[3], 1, 3)
+        xa_q = [quantize(xa_bf0, "xa0")]
+        xa_bf1 = interleave(vessel1, "scalar", "xa_bf")
+
+        ridge1 = [kept([P, PACK, c1 - c0], F32, f"ridge1_{c0}") for c0, c1 in PIECES]
+        ridge1_bf = [kept([P, PACK, c1 - c0], BF16, f"ridge1_bf_{c0}") for c0, c1 in PIECES]
+
+        def ridge_piece(i):
+            c0, c1 = PIECES[i]
+            for t in range(PACK):
+                pick_ridge(ridge1[i], h1[t], t, c0, c1)
+                if t > 0:
+                    bound_ridge(ridge1_bf[i], ridge1[i], 1, t - 1)
+            bound_ridge(ridge1_bf[i], ridge1[i], 1, PACK - 1)
+            return interleave(ridge1_bf[i], "scalar", "xb_bf")
+
+        xb_q0 = quantize(xb_bf0, "xb0")
+        xb_bf1 = [ridge_piece(0)]
+        xa_q.append(quantize(xa_bf1, "xa1"))
+
+        ya = kept([P, PACK, NPAIR], F32, "ya")
+        for t in range(PACK):
+            bank = psum.tile([P, BANK], F32, name="bank", tag="bank")
+            for a in range(2):
+                nc.tensor.matmul_mx(
+                    out=bank[:],
+                    lhsT=wa_codes[:, a, 2 * t * P : 2 * (t + 1) * P].bitcast(FP4X4),
+                    lhsT_scale=wa_sc[:, a, t * P : (t + 1) * P],
+                    rhs=xa_q[a][0][:].bitcast(FP8X4),
+                    rhs_scale=xa_q[a][1][:],
+                    start=(a == 0),
+                    stop=(a == 1),
+                )
+            nc.scalar.copy(out=ya[:, t, :], in_=bank[:])
+
+        for i in range(1, len(PIECES)):
+            xb_bf1.append(ridge_piece(i))
+
+        y_codes = kept([P, NPAIR], U32, "y_codes")
+        y_scales = kept([P, NPAIR], U8, "y_scales")
+        out_rows = out_0.rearrange("(p t) m -> p t m", t=PACK)
+        out_words = out_1[0].rearrange("p m t -> p (m t)").bitcast(I32)
+        for i, (c0, c1) in enumerate(PIECES):
+            width = c1 - c0
+            per_bank = BANK // width
+            xb_q1 = quantize(xb_bf1[i], f"xb1_{c0}")
+            y = kept([P, PACK, width], F32, f"y_{c0}")
+            for t0 in range(0, PACK, per_bank):
+                bank = psum.tile([P, per_bank, width], F32, name="bank", tag="bank")
+                for a in range(2):
+                    codes = xb_q0[0][:, c0:c1] if a == 0 else xb_q1[0][:]
+                    scales = xb_q0[1][:, c0:c1] if a == 0 else xb_q1[1][:]
+                    for u in range(per_bank):
+                        cols = slice((t0 + u) * P, (t0 + u + 1) * P)
+                        nc.tensor.matmul_mx(
+                            out=bank[:, u, :],
+                            lhsT=wb_q[a][0][:, cols].bitcast(FP8X4),
+                            lhsT_scale=wb_q[a][1][:, cols],
+                            rhs=codes.bitcast(FP8X4),
+                            rhs_scale=scales,
+                            start=(a == 0 and u == 0),
+                            stop=(a == 1 and u == per_bank - 1),
+                        )
+                nc.vector.tensor_tensor(
+                    out=y[:, t0 : t0 + per_bank, :], in0=bank[:], in1=ya[:, t0 : t0 + per_bank, c0:c1], op=MULT
+                )
+            nc.sync.dma_start(out=out_rows[:, :, c0:c1], in_=y[:])
+            y_bf = interleave(y, "vector" if i == len(PIECES) - 1 else "scalar", "y_bf")
+            nc.vector.quantize_mx(out=y_codes[:, c0:c1].bitcast(FP8X4), scales=y_scales[:, c0:c1], in_=y_bf[:])
+            nc.sync.dma_start(out=out_words[:, c0:c1], in_=y_codes[:, c0:c1].bitcast(I32))
+        for q in range(4):
+            queue = nc.sync if q % 2 == 0 else nc.scalar
+            queue.dma_start(
+                out=out_2[0, 4 * q : 4 * q + 4, :].bitcast(I32), in_=y_scales[32 * q : 32 * q + 4, :].bitcast(I32)
+            )

@@ -21,7 +21,7 @@ P = 128
 PACK = 4
 KP = P * PACK
 BANK = 512
-PIECES = ((0, 256), (256, 512))
+HALF = NPAIR // 2
 HEAD_SPLIT = 84
 
 
@@ -31,15 +31,11 @@ def tile_list_rop_vessel_ridge_kernel(
     nc = tc.nc
     with ExitStack() as ctx:
         lists = ctx.enter_context(tc.tile_pool(name="lists", bufs=1))
-        keep = ctx.enter_context(tc.tile_pool(name="keep", bufs=1))
-        ring = ctx.enter_context(tc.tile_pool(name="ring", bufs=4))
+        sb = ctx.enter_context(tc.tile_pool(name="sb", bufs=1))
         psum = ctx.enter_context(tc.psum_pool(name="psum", bufs=8))
 
-        def kept(shape, dtype, name):
-            return keep.tile(shape, dtype, name=name, align_bytes=64)
-
-        def staged(width, name):
-            return ring.tile([P, width], BF16, name=name, tag="staged", align_bytes=64)
+        def tile(shape, dtype, name, slot=None):
+            return sb.tile(shape, dtype, name=name, tag=slot or name, align_bytes=64)
 
         def copy_on(engine, out, in_):
             if engine == "vector":
@@ -52,36 +48,25 @@ def tile_list_rop_vessel_ridge_kernel(
         pos2_t = lists.tile([P, NPAIR // 16], U16, name="pos2_t")
         nc.sync.dma_start(offs_t[:], offs)
 
-        scale_window = kept([P, T], U8, "scale_window")
-        nc.vector.memset(scale_window[:].bitcast(I32), 0)
-        nc.gpsimd.dma_start(
-            out=scale_window[0:P:4, :].bitcast(I32),
-            in_=tab_scales.rearrange("a q t -> (a q) t").bitcast(I32),
-        )
+        scale_window = [tile([P, T], U8, f"scale_window{a}", ("load_a", "v_codes0")[a]) for a in range(2)]
+        for a in range(2):
+            nc.vector.memset(scale_window[a][:].bitcast(I32), 0)
+            nc.scalar.dma_start(out=scale_window[a][0:P:8, :].bitcast(I32), in_=tab_scales[a].bitcast(I32))
 
-        table = [kept([P, T], U32, f"table{a}") for a in range(2)]
-        nc.sync.dma_start(out=table[0][:].bitcast(I32), in_=tab_words[0].rearrange("p t i -> p (t i)").bitcast(I32))
-        wa_raw = kept([P, 2, 2 * N], U8, "wa_raw")
+        wa_raw = tile([P, 2, 2 * N], U8, "wa_raw", "load_c")
         nc.sync.dma_start(out=wa_raw[:].bitcast(I32), in_=wa_words.rearrange("a p c -> p a c").bitcast(I32))
-        nc.sync.dma_start(out=table[1][:].bitcast(I32), in_=tab_words[1].rearrange("p t i -> p (t i)").bitcast(I32))
 
-        def load_weight(w, a, b):
-            raw = ring.tile([P, PACK, KP], F32, name="raw", tag="raw")
-            nc.sync.dma_start(
-                out=raw[:], in_=w[a * KP : (a + 1) * KP, b * KP : (b + 1) * KP].rearrange("(p j) c -> p j c", j=PACK)
-            )
-            return raw
+        def load_table(a, slot):
+            words = tile([P, T], U32, f"table{a}", slot)
+            nc.sync.dma_start(out=words[:].bitcast(I32), in_=tab_words[a].rearrange("p t i -> p (t i)").bitcast(I32))
+            return words
 
-        w1_raw = {}
-        w1_raw[0, 0] = load_weight(w1, 0, 0)
-        w1_raw[1, 0] = load_weight(w1, 1, 0)
+        table = [load_table(0, "load_b")]
         nc.sync.dma_start(pos1_t[:], pos1)
         nc.sync.dma_start(pos2_t[:], pos2)
-        w1_raw[0, 1] = load_weight(w1, 0, 1)
-        w1_raw[1, 1] = load_weight(w1, 1, 1)
 
         def load_vector(v, name):
-            t = kept([P, 2, PACK], F32, name)
+            t = tile([P, 2, PACK], F32, name)
             nc.scalar.dma_start(out=t[:], in_=v.rearrange("(b p t) -> p b t", b=2, t=PACK))
             return t
 
@@ -90,60 +75,74 @@ def tile_list_rop_vessel_ridge_kernel(
         b1_t = load_vector(b1, "b1_t")
         cb_t = load_vector(cb, "cb_t")
 
-        was_raw = kept([P, 2, N], U8, "was_raw")
-        nc.vector.memset(was_raw[:].bitcast(I32), 0)
-        for q in range(4):
-            nc.scalar.dma_start(
-                out=was_raw[32 * q : 32 * q + 4, :, :].bitcast(I32),
-                in_=wa_scales[:, 4 * q : 4 * q + 4, :].rearrange("a r c -> r a c").bitcast(I32),
+        def load_rows(dst, w, a, b):
+            nc.sync.dma_start(
+                out=dst, in_=w[a * KP : (a + 1) * KP, b * KP : (b + 1) * KP].rearrange("(p j) c -> p j c", j=PACK)
             )
 
-        picked_scales = kept([P, S], U8, "picked_scales")
-        nc.vector.tensor_copy(out=picked_scales[:], in_=scale_window[:].indirect(offs_t[:]))
-        v_scales = kept([P, 2, S], U8, "v_scales")
-        nc.vector.memset(v_scales[:].bitcast(I32), 0)
-        for a in range(2):
-            for q in range(4):
-                first = 64 * a + 16 * q
-                nc.gpsimd.dma_start(
-                    out=v_scales[32 * q : 32 * q + 4, a, :].bitcast(I32),
-                    in_=picked_scales[first : first + 16 : 4, :].bitcast(I32),
-                )
+        def load_w1(a, b, slot):
+            raw = tile([P, PACK, KP], F32, f"w1_raw{a}{b}", slot)
+            load_rows(raw[:], w1, a, b)
+            return raw
 
-        gain_va = kept([P, 2, PACK], F32, "gain_va")
-        nc.vector.tensor_tensor(out=gain_va[:], in0=gain_t[:], in1=va_t[:], op=MULT)
-        spread = kept([P, 2, PACK, NPAIR], F32, "spread")
-        for b in range(2):
-            for t in range(PACK):
-                nc.scalar.copy(out=spread[:, b, t, :], in_=gain_va[:, b, t : t + 1].to_broadcast([P, NPAIR]))
-
-        v_codes = [kept([P, S], U32, f"v_codes{a}") for a in range(2)]
-        nc.vector.tensor_copy(out=v_codes[0][:], in_=table[0][:].indirect(offs_t[:]))
-
-        wa_codes = kept([P, 2, 2 * N], U8, "wa_codes")
+        wa_codes = tile([P, 2, 2 * N], U8, "wa_codes")
         nc.vector.tensor_copy(
             out=wa_codes[:].rearrange("p a (t m e) -> p a m t e", t=PACK, e=2),
             in_=wa_raw[:].rearrange("p a (m t e) -> p a m t e", t=PACK, e=2),
         )
-        wa_sc = kept([P, 2, N], U8, "wa_sc")
-        nc.vector.tensor_copy(
-            out=wa_sc[:].rearrange("p a (t m) -> p a m t", t=PACK),
-            in_=was_raw[:].rearrange("p a (m t) -> p a m t", t=PACK),
-        )
+        table.append(load_table(1, "load_c"))
+
+        picked_scales = tile([P, 2, S], U8, "picked_scales", "small")
+        for a in range(2):
+            nc.vector.tensor_copy(out=picked_scales[:, a, :], in_=scale_window[a][:].indirect(offs_t[:]))
+        v_scales = tile([P, 2, S], U8, "v_scales")
+        nc.gpsimd.memset(v_scales[:].bitcast(I32), 0)
+        for q in range(4):
+            nc.scalar.dma_start(
+                out=v_scales[32 * q : 32 * q + 4, :, :].bitcast(I32),
+                in_=picked_scales[32 * q : 32 * (q + 1) : 8, :, :].bitcast(I32),
+            )
+        w1_raw = {(0, 0): load_w1(0, 0, "load_a")}
+
+        gain_va = tile([P, 2, PACK], F32, "gain_va")
+        nc.vector.tensor_tensor(out=gain_va[:], in0=gain_t[:], in1=va_t[:], op=MULT)
+        spread = tile([P, 2, PACK, NPAIR], F32, "spread")
+        for b in range(2):
+            for t in range(PACK):
+                nc.scalar.copy(out=spread[:, b, t, :], in_=gain_va[:, b, t : t + 1].to_broadcast([P, NPAIR]))
+
+        v_codes = [tile([P, S], U32, f"v_codes{a}") for a in range(2)]
+        nc.vector.tensor_copy(out=v_codes[0][:], in_=table[0][:].indirect(offs_t[:]))
+        last_raw = tile([P, 2, PACK, KP // 2], F32, "last_raw", "load_b")
+        for u in range(2):
+            nc.sync.dma_start(
+                out=last_raw[:, u],
+                in_=w1[KP : 2 * KP, u * KP // 2 : (u + 1) * KP // 2].rearrange("(p j) c -> p j c", j=PACK),
+            )
         nc.vector.tensor_copy(out=v_codes[1][:], in_=table[1][:].indirect(offs_t[:]))
+        w1_raw[0, 1] = load_w1(0, 1, "load_c")
+
+
+        was_raw = tile([P, 2, N], U8, "was_raw", "small")
+        nc.gpsimd.memset(was_raw[:].bitcast(I32), 0)
+        for q in range(4):
+            nc.sync.dma_start(
+                out=was_raw[32 * q : 32 * q + 4, :, :].bitcast(I32),
+                in_=wa_scales[:, 4 * q : 4 * q + 4, :].rearrange("a r c -> r a c").bitcast(I32),
+            )
 
         def round_weight(raw, shares, name):
-            rounded = staged(PACK * KP, name)
+            rounded = tile([P, PACK * KP], BF16, name)
             dst = rounded[:].rearrange("p (t m j) -> p m j t", t=PACK, j=PACK)
-            src = raw[:].rearrange("p j (m t) -> p m j t", t=PACK)
+            src = raw.rearrange("p j (m t) -> p m j t", t=PACK)
             for engine, m0, m1 in shares:
                 copy_on(engine, dst[:, m0:m1], src[:, m0:m1])
             return rounded
 
         def quantize(rounded, name, parts=1):
             width = rounded.shape[1] // PACK
-            codes = kept([P, width], U32, name + "_codes")
-            scales = kept([P, width], U8, name + "_scales")
+            codes = tile([P, width], U32, name + "_codes")
+            scales = tile([P, width], U8, name + "_scales")
             step = width // parts
             for c in range(0, width, step):
                 nc.vector.quantize_mx(
@@ -154,14 +153,22 @@ def tile_list_rop_vessel_ridge_kernel(
             return codes, scales
 
         both = (("vector", 0, HEAD_SPLIT), ("scalar", HEAD_SPLIT, P))
+        on_vector = (("vector", 0, P),)
+        on_scalar = (("scalar", 0, P),)
         w1_q = {}
-        for a in range(2):
-            w1_q[a, 0] = quantize(round_weight(w1_raw[a, 0], both, "w1_bf"), f"w1_{a}0", parts=1 + a)
-
-        wb_raw = [load_weight(wb, a, 0) for a in range(2)]
+        w1_q[0, 0] = quantize(round_weight(w1_raw[0, 0][:], both, "w1_bf00"), "w1_00")
+        w1_raw[1, 1] = load_w1(1, 1, "load_a")
+        last_bf = tile([P, PACK * KP], BF16, "w1_bf10")
+        for u, engine in enumerate(("scalar", "vector")):
+            copy_on(
+                engine,
+                last_bf[:].rearrange("p (t m j) -> p m j t", t=PACK, j=PACK)[:, u * P // 2 : (u + 1) * P // 2],
+                last_raw[:, u].rearrange("p j (m t) -> p m j t", t=PACK),
+            )
+        w1_q[1, 0] = quantize(last_bf, "w1_10", parts=2)
 
         def first_stage(b, t):
-            h = ring.tile([P, S], F32, name="h", tag="h", bufs=8)
+            h = tile([P, S], F32, f"h{b}{t}")
             cols = slice(t * P, (t + 1) * P)
             for half in range(S // BANK):
                 picks = slice(half * BANK, (half + 1) * BANK)
@@ -182,21 +189,21 @@ def tile_list_rop_vessel_ridge_kernel(
         def pick_vessel(dst, h, b, t):
             nc.vector.tensor_tensor(out=dst[:, t, :], in0=h[:].indirect(pos1_t[:]), in1=spread[:, b, t, :], op=MULT)
 
-        def pick_ridge(dst, h, t, c0, c1):
-            nc.vector.tensor_copy(out=dst[:, t, :], in_=h[:].indirect(pos2_t[:, c0 // 16 : c1 // 16]))
+        def pick_ridge(dst, h, c0, c1):
+            nc.vector.tensor_copy(out=dst, in_=h[:].indirect(pos2_t[:, c0 // 16 : c1 // 16]))
 
         def bound_ridge(dst, src, b, t):
             nc.vector.tensor_scalar(
-                out=dst[:, t, :],
-                in0=src[:, t, :],
+                out=dst,
+                in0=src,
                 scalar1=gain_t[:, b, t : t + 1],
                 scalar2=cb_t[:, b, t : t + 1],
                 op0=MULT,
                 op1=MAX,
             )
 
-        def interleave(src, engine, name):
-            woven = staged(PACK * src.shape[2], name)
+        def interleave(src, engine, name, slot=None):
+            woven = tile([P, PACK * src.shape[2]], BF16, name, slot)
             copy_on(
                 engine,
                 woven[:].rearrange("p (c i t) -> p c t i", i=4, t=PACK),
@@ -204,53 +211,56 @@ def tile_list_rop_vessel_ridge_kernel(
             )
             return woven
 
-        h0 = [first_stage(0, t) for t in range(PACK)]
-        w1_bf = [round_weight(w1_raw[a, 1], (("scalar", 0, P),), "w1_bf") for a in range(2)]
+        vessel0 = tile([P, PACK, NPAIR], F32, "vessel0")
+        ridge0 = tile([P, PACK, NPAIR], F32, "ridge0")
+        ridge0_bf = tile([P, PACK, NPAIR], BF16, "ridge0_bf")
 
-        vessel0 = kept([P, PACK, NPAIR], F32, "vessel0")
-        ridge0 = kept([P, PACK, NPAIR], F32, "ridge0")
-        ridge0_bf = kept([P, PACK, NPAIR], BF16, "ridge0_bf")
-        for t in range(PACK):
-            pick_vessel(vessel0, h0[t], 0, t)
+        def pick_both(t):
+            h = first_stage(0, t)
+            pick_vessel(vessel0, h, 0, t)
             if t > 0:
-                bound_ridge(ridge0_bf, ridge0, 0, t - 1)
-            if t >= 2:
-                w1_q[t - 2, 1] = quantize(w1_bf[t - 2], f"w1_{t - 2}1")
-            pick_ridge(ridge0, h0[t], t, 0, NPAIR)
-        h1 = [first_stage(1, t) for t in range(PACK)]
-        wb_bf0 = round_weight(wb_raw[0], (("vector", 0, P),), "wb_bf")
-        bound_ridge(ridge0_bf, ridge0, 0, PACK - 1)
-        xa_bf0 = interleave(vessel0, "scalar", "xa_bf")
-        xb_bf0 = interleave(ridge0_bf, "scalar", "xb_bf")
+                bound_ridge(ridge0_bf[:, t - 1, :], ridge0[:, t - 1, :], 0, t - 1)
+            pick_ridge(ridge0[:, t, :], h, 0, NPAIR)
 
-        vessel1 = kept([P, PACK, NPAIR], F32, "vessel1")
-        pick_vessel(vessel1, h1[0], 1, 0)
-        wb_q = [quantize(wb_bf0, "wb0")]
-        pick_vessel(vessel1, h1[1], 1, 1)
-        wb_bf1 = round_weight(wb_raw[1], (("vector", 0, P),), "wb_bf")
-        pick_vessel(vessel1, h1[2], 1, 2)
-        wb_q.append(quantize(wb_bf1, "wb1"))
-        pick_vessel(vessel1, h1[3], 1, 3)
-        xa_q = [quantize(xa_bf0, "xa0")]
-        xa_bf1 = interleave(vessel1, "scalar", "xa_bf")
+        pick_both(0)
+        pick_both(1)
+        w1_q[0, 1] = quantize(round_weight(w1_raw[0, 1][:], on_scalar, "w1_bf01"), "w1_01")
+        pick_both(2)
+        w1_q[1, 1] = quantize(round_weight(w1_raw[1, 1][:], on_scalar, "w1_bf11"), "w1_11")
+        wb_raw = tile([P, 2, PACK, KP], F32, "wb_raw", "load_a")
+        for a in range(2):
+            load_rows(wb_raw[:, a], wb, a, 0)
+        pick_both(3)
+        wa_sc = tile([P, 2, N], U8, "wa_sc", "h02")
+        nc.vector.tensor_copy(
+            out=wa_sc[:].rearrange("p a (t m) -> p a m t", t=PACK),
+            in_=was_raw[:].rearrange("p a (m t) -> p a m t", t=PACK),
+        )
+        bound_ridge(ridge0_bf[:, PACK - 1, :], ridge0[:, PACK - 1, :], 0, PACK - 1)
 
-        ridge1 = [kept([P, PACK, c1 - c0], F32, f"ridge1_{c0}") for c0, c1 in PIECES]
-        ridge1_bf = [kept([P, PACK, c1 - c0], BF16, f"ridge1_bf_{c0}") for c0, c1 in PIECES]
+        vessel1 = tile([P, PACK, NPAIR], F32, "vessel1")
+        h1 = []
+        for t in range(PACK):
+            h1.append(first_stage(1, t))
+            pick_vessel(vessel1, h1[t], 1, t)
+        wb_q = [quantize(round_weight(wb_raw[:, a], on_vector, f"wb_bf{a}"), f"wb{a}") for a in range(2)]
+        xa_q = [quantize(interleave(vessel0, "scalar", "xa_bf0"), "xa0")]
+        xa_q.append(quantize(interleave(vessel1, "scalar", "xa_bf1", "gate0"), "xa1"))
 
-        def ridge_piece(i):
-            c0, c1 = PIECES[i]
-            for t in range(PACK):
-                pick_ridge(ridge1[i], h1[t], t, c0, c1)
-                if t > 0:
-                    bound_ridge(ridge1_bf[i], ridge1[i], 1, t - 1)
-            bound_ridge(ridge1_bf[i], ridge1[i], 1, PACK - 1)
-            return interleave(ridge1_bf[i], "scalar", "xb_bf")
+        def ridge_rows(bounded, i, t0, t1, slot):
+            picked = tile([P, t1 - t0, HALF], F32, f"ridge1_{i}{t0}", slot)
+            for t in range(t0, t1):
+                pick_ridge(picked[:, t - t0, :], h1[t], i * HALF, (i + 1) * HALF)
+                if t > t0:
+                    bound_ridge(bounded[:, t - 1, :], picked[:, t - 1 - t0, :], 1, t - 1)
+            bound_ridge(bounded[:, t1 - 1, :], picked[:, t1 - 1 - t0, :], 1, t1 - 1)
 
+        xb_bf0 = interleave(ridge0_bf, "scalar", "xb_bf0", "gate1")
+        bounded = [tile([P, PACK, HALF], BF16, f"ridge1_bf{i}") for i in range(2)]
+        ridge_rows(bounded[0], 0, 0, PACK, "gate0")
         xb_q0 = quantize(xb_bf0, "xb0")
-        xb_bf1 = [ridge_piece(0)]
-        xa_q.append(quantize(xa_bf1, "xa1"))
 
-        ya = kept([P, PACK, NPAIR], F32, "ya")
+        ya = tile([P, PACK, NPAIR], F32, "ya")
         for t in range(PACK):
             bank = psum.tile([P, BANK], F32, name="bank", tag="bank")
             for a in range(2):
@@ -265,23 +275,27 @@ def tile_list_rop_vessel_ridge_kernel(
                 )
             nc.scalar.copy(out=ya[:, t, :], in_=bank[:])
 
-        for i in range(1, len(PIECES)):
-            xb_bf1.append(ridge_piece(i))
+        xb_bf10 = interleave(bounded[0], "scalar", "xb_bf10", "gate2")
+        ridge_rows(bounded[1], 1, 0, 2, "gate1")
+        xb_q1 = [quantize(xb_bf10, "xb1_0")]
+        ridge_rows(bounded[1], 1, 2, PACK, "gate2")
+        xb_bf11 = interleave(bounded[1], "scalar", "xb_bf11")
 
-        y_codes = kept([P, NPAIR], U32, "y_codes")
-        y_scales = kept([P, NPAIR], U8, "y_scales")
+        y_codes = tile([P, NPAIR], U32, "y_codes")
+        y_scales = tile([P, NPAIR], U8, "y_scales")
         out_rows = out_0.rearrange("(p t) m -> p t m", t=PACK)
         out_words = out_1[0].rearrange("p m t -> p (m t)").bitcast(I32)
-        for i, (c0, c1) in enumerate(PIECES):
-            width = c1 - c0
-            per_bank = BANK // width
-            xb_q1 = quantize(xb_bf1[i], f"xb1_{c0}")
-            y = kept([P, PACK, width], F32, f"y_{c0}")
+        per_bank = BANK // HALF
+        for i in range(2):
+            pairs = slice(i * HALF, (i + 1) * HALF)
+            if i == 1:
+                xb_q1.append(quantize(xb_bf11, "xb1_1"))
+            y = tile([P, PACK, HALF], F32, f"y_{i}")
             for t0 in range(0, PACK, per_bank):
-                bank = psum.tile([P, per_bank, width], F32, name="bank", tag="bank")
+                bank = psum.tile([P, per_bank, HALF], F32, name="bank", tag="bank")
                 for a in range(2):
-                    codes = xb_q0[0][:, c0:c1] if a == 0 else xb_q1[0][:]
-                    scales = xb_q0[1][:, c0:c1] if a == 0 else xb_q1[1][:]
+                    codes = xb_q0[0][:, pairs] if a == 0 else xb_q1[i][0][:]
+                    scales = xb_q0[1][:, pairs] if a == 0 else xb_q1[i][1][:]
                     for u in range(per_bank):
                         cols = slice((t0 + u) * P, (t0 + u + 1) * P)
                         nc.tensor.matmul_mx(
@@ -294,12 +308,12 @@ def tile_list_rop_vessel_ridge_kernel(
                             stop=(a == 1 and u == per_bank - 1),
                         )
                 nc.vector.tensor_tensor(
-                    out=y[:, t0 : t0 + per_bank, :], in0=bank[:], in1=ya[:, t0 : t0 + per_bank, c0:c1], op=MULT
+                    out=y[:, t0 : t0 + per_bank, :], in0=bank[:], in1=ya[:, t0 : t0 + per_bank, pairs], op=MULT
                 )
-            nc.sync.dma_start(out=out_rows[:, :, c0:c1], in_=y[:])
-            y_bf = interleave(y, "vector" if i == len(PIECES) - 1 else "scalar", "y_bf")
-            nc.vector.quantize_mx(out=y_codes[:, c0:c1].bitcast(FP8X4), scales=y_scales[:, c0:c1], in_=y_bf[:])
-            nc.sync.dma_start(out=out_words[:, c0:c1], in_=y_codes[:, c0:c1].bitcast(I32))
+            nc.sync.dma_start(out=out_rows[:, :, pairs], in_=y[:])
+            y_bf = interleave(y, ("scalar", "vector")[i], f"y_bf{i}")
+            nc.vector.quantize_mx(out=y_codes[:, pairs].bitcast(FP8X4), scales=y_scales[:, pairs], in_=y_bf[:])
+            nc.sync.dma_start(out=out_words[:, pairs], in_=y_codes[:, pairs].bitcast(I32))
         for q in range(4):
             queue = nc.sync if q % 2 == 0 else nc.scalar
             queue.dma_start(

@@ -22,7 +22,9 @@ PACK = 4
 KP = P * PACK
 BANK = 512
 HALF = NPAIR // 2
-HEAD_SPLIT = 84
+HEAD_SPLIT = 44
+SYNC_MOVES = 5
+TAIL_HELP = 20
 
 
 def tile_list_rop_vessel_ridge_kernel(
@@ -32,7 +34,7 @@ def tile_list_rop_vessel_ridge_kernel(
     with ExitStack() as ctx:
         lists = ctx.enter_context(tc.tile_pool(name="lists", bufs=1))
         sb = ctx.enter_context(tc.tile_pool(name="sb", bufs=1))
-        psum = ctx.enter_context(tc.psum_pool(name="psum", bufs=8))
+        psum = ctx.enter_context(tc.psum_pool(name="psum", bufs=4))
 
         def tile(shape, dtype, name, slot=None):
             return sb.tile(shape, dtype, name=name, tag=slot or name, align_bytes=64)
@@ -48,13 +50,24 @@ def tile_list_rop_vessel_ridge_kernel(
         pos2_t = lists.tile([P, NPAIR // 16], U16, name="pos2_t")
         nc.sync.dma_start(offs_t[:], offs)
 
-        scale_window = [tile([P, T], U8, f"scale_window{a}", ("load_a", "v_codes0")[a]) for a in range(2)]
-        for a in range(2):
-            nc.vector.memset(scale_window[a][:].bitcast(I32), 0)
-            nc.scalar.dma_start(out=scale_window[a][0:P:8, :].bitcast(I32), in_=tab_scales[a].bitcast(I32))
+        was_raw = tile([P, 2, N], U8, "was_raw")
+        nc.gpsimd.memset(was_raw[:].bitcast(I32), 0)
+        for q in range(4):
+            nc.scalar.dma_start(
+                out=was_raw[32 * q : 32 * q + 4, :, :].bitcast(I32),
+                in_=wa_scales[:, 4 * q : 4 * q + 4, :].rearrange("a r c -> r a c").bitcast(I32),
+            )
+        scale_window = tile([P, T], U8, "scale_window")
+        nc.vector.memset(scale_window[:].bitcast(I32), 0)
+        nc.scalar.dma_start(
+            out=scale_window[0:P:4, :].bitcast(I32), in_=tab_scales.rearrange("a q t -> (a q) t").bitcast(I32)
+        )
+        nc.sync.dma_start(pos1_t[:], pos1)
+        nc.sync.dma_start(pos2_t[:], pos2)
 
-        wa_raw = tile([P, 2, 2 * N], U8, "wa_raw", "load_c")
-        nc.sync.dma_start(out=wa_raw[:].bitcast(I32), in_=wa_words.rearrange("a p c -> p a c").bitcast(I32))
+        wa_raw = [tile([P, 2 * N], U8, f"wa_raw{a}", ("load_c", "load_a")[a]) for a in range(2)]
+        for a in range(2):
+            nc.sync.dma_start(out=wa_raw[a][:].bitcast(I32), in_=wa_words[a].bitcast(I32))
 
         def load_table(a, slot):
             words = tile([P, T], U32, f"table{a}", slot)
@@ -62,12 +75,10 @@ def tile_list_rop_vessel_ridge_kernel(
             return words
 
         table = [load_table(0, "load_b")]
-        nc.sync.dma_start(pos1_t[:], pos1)
-        nc.sync.dma_start(pos2_t[:], pos2)
 
         def load_vector(v, name):
             t = tile([P, 2, PACK], F32, name)
-            nc.scalar.dma_start(out=t[:], in_=v.rearrange("(b p t) -> p b t", b=2, t=PACK))
+            nc.gpsimd.dma_start(out=t[:], in_=v.rearrange("(b p t) -> p b t", b=2, t=PACK))
             return t
 
         gain_t = load_vector(gain, "gain_t")
@@ -86,30 +97,40 @@ def tile_list_rop_vessel_ridge_kernel(
             return raw
 
         wa_codes = tile([P, 2, 2 * N], U8, "wa_codes")
-        nc.vector.tensor_copy(
-            out=wa_codes[:].rearrange("p a (t m e) -> p a m t e", t=PACK, e=2),
-            in_=wa_raw[:].rearrange("p a (m t e) -> p a m t e", t=PACK, e=2),
-        )
-        table.append(load_table(1, "load_c"))
-
-        picked_scales = tile([P, 2, S], U8, "picked_scales", "small")
         for a in range(2):
-            nc.vector.tensor_copy(out=picked_scales[:, a, :], in_=scale_window[a][:].indirect(offs_t[:]))
-        v_scales = tile([P, 2, S], U8, "v_scales")
-        nc.gpsimd.memset(v_scales[:].bitcast(I32), 0)
-        for q in range(4):
-            nc.scalar.dma_start(
-                out=v_scales[32 * q : 32 * q + 4, :, :].bitcast(I32),
-                in_=picked_scales[32 * q : 32 * (q + 1) : 8, :, :].bitcast(I32),
+            nc.vector.tensor_copy(
+                out=wa_codes[:, a].rearrange("p (t m e) -> p m t e", t=PACK, e=2),
+                in_=wa_raw[a][:].rearrange("p (m t e) -> p m t e", t=PACK, e=2),
             )
+        table.append(load_table(1, "load_c"))
         w1_raw = {(0, 0): load_w1(0, 0, "load_a")}
 
+        wa_sc = tile([P, 2, N], U8, "wa_sc")
+        nc.vector.tensor_copy(
+            out=wa_sc[:].rearrange("p a (t m) -> p a m t", t=PACK),
+            in_=was_raw[:].rearrange("p a (m t) -> p a m t", t=PACK),
+        )
+
+        picked_scales = tile([P, S], U8, "picked_scales")
+        nc.vector.tensor_copy(out=picked_scales[:], in_=scale_window[:].indirect(offs_t[:]))
+        v_scales = tile([P, 2, S], U8, "v_scales")
+        nc.vector.memset(v_scales[:].bitcast(I32), 0)
+
         gain_va = tile([P, 2, PACK], F32, "gain_va")
-        nc.vector.tensor_tensor(out=gain_va[:], in0=gain_t[:], in1=va_t[:], op=MULT)
+        nc.gpsimd.tensor_tensor(out=gain_va[:], in0=gain_t[:], in1=va_t[:], op=MULT)
         spread = tile([P, 2, PACK, NPAIR], F32, "spread")
         for b in range(2):
             for t in range(PACK):
                 nc.scalar.copy(out=spread[:, b, t, :], in_=gain_va[:, b, t : t + 1].to_broadcast([P, NPAIR]))
+
+        for a in range(2):
+            for q in range(4):
+                first = 64 * a + 16 * q
+                queue = nc.sync if 4 * a + q < SYNC_MOVES else nc.gpsimd
+                queue.dma_start(
+                    out=v_scales[32 * q : 32 * q + 4, a, :].bitcast(I32),
+                    in_=picked_scales[first : first + 16 : 4, :].bitcast(I32),
+                )
 
         v_codes = [tile([P, S], U32, f"v_codes{a}") for a in range(2)]
         nc.vector.tensor_copy(out=v_codes[0][:], in_=table[0][:].indirect(offs_t[:]))
@@ -122,14 +143,6 @@ def tile_list_rop_vessel_ridge_kernel(
         nc.vector.tensor_copy(out=v_codes[1][:], in_=table[1][:].indirect(offs_t[:]))
         w1_raw[0, 1] = load_w1(0, 1, "load_c")
 
-
-        was_raw = tile([P, 2, N], U8, "was_raw", "small")
-        nc.gpsimd.memset(was_raw[:].bitcast(I32), 0)
-        for q in range(4):
-            nc.sync.dma_start(
-                out=was_raw[32 * q : 32 * q + 4, :, :].bitcast(I32),
-                in_=wa_scales[:, 4 * q : 4 * q + 4, :].rearrange("a r c -> r a c").bitcast(I32),
-            )
 
         def round_weight(raw, shares, name):
             rounded = tile([P, PACK * KP], BF16, name)
@@ -156,7 +169,7 @@ def tile_list_rop_vessel_ridge_kernel(
         on_vector = (("vector", 0, P),)
         on_scalar = (("scalar", 0, P),)
         w1_q = {}
-        w1_q[0, 0] = quantize(round_weight(w1_raw[0, 0][:], both, "w1_bf00"), "w1_00")
+        w1_q[0, 0] = quantize(round_weight(w1_raw[0, 0][:], both, "w1_bf00"), "w1_00", parts=2)
         w1_raw[1, 1] = load_w1(1, 1, "load_a")
         last_bf = tile([P, PACK * KP], BF16, "w1_bf10")
         for u, engine in enumerate(("scalar", "vector")):
@@ -172,7 +185,7 @@ def tile_list_rop_vessel_ridge_kernel(
             cols = slice(t * P, (t + 1) * P)
             for half in range(S // BANK):
                 picks = slice(half * BANK, (half + 1) * BANK)
-                bank = psum.tile([P, BANK], F32, name="bank", tag="bank")
+                bank = psum.tile([P, BANK], F32, name="bank", tag="bank", bufs=3)
                 for a in range(2):
                     nc.tensor.matmul_mx(
                         out=bank[:],
@@ -202,13 +215,13 @@ def tile_list_rop_vessel_ridge_kernel(
                 op1=MAX,
             )
 
-        def interleave(src, engine, name, slot=None):
+        def interleave(src, engine, name, slot=None, helped=0):
             woven = tile([P, PACK * src.shape[2]], BF16, name, slot)
-            copy_on(
-                engine,
-                woven[:].rearrange("p (c i t) -> p c t i", i=4, t=PACK),
-                src[:].rearrange("p t (c i) -> p c t i", i=4),
-            )
+            dst = woven[:].rearrange("p (c i t) -> p c t i", i=4, t=PACK)
+            rows = src[:].rearrange("p t (c i) -> p c t i", i=4)
+            copy_on(engine, dst[:, helped:], rows[:, helped:])
+            if helped:
+                copy_on("scalar", dst[:, :helped], rows[:, :helped])
             return woven
 
         vessel0 = tile([P, PACK, NPAIR], F32, "vessel0")
@@ -223,19 +236,14 @@ def tile_list_rop_vessel_ridge_kernel(
             pick_ridge(ridge0[:, t, :], h, 0, NPAIR)
 
         pick_both(0)
-        pick_both(1)
         w1_q[0, 1] = quantize(round_weight(w1_raw[0, 1][:], on_scalar, "w1_bf01"), "w1_01")
-        pick_both(2)
+        pick_both(1)
         w1_q[1, 1] = quantize(round_weight(w1_raw[1, 1][:], on_scalar, "w1_bf11"), "w1_11")
         wb_raw = tile([P, 2, PACK, KP], F32, "wb_raw", "load_a")
         for a in range(2):
             load_rows(wb_raw[:, a], wb, a, 0)
+        pick_both(2)
         pick_both(3)
-        wa_sc = tile([P, 2, N], U8, "wa_sc", "h02")
-        nc.vector.tensor_copy(
-            out=wa_sc[:].rearrange("p a (t m) -> p a m t", t=PACK),
-            in_=was_raw[:].rearrange("p a (m t) -> p a m t", t=PACK),
-        )
         bound_ridge(ridge0_bf[:, PACK - 1, :], ridge0[:, PACK - 1, :], 0, PACK - 1)
 
         vessel1 = tile([P, PACK, NPAIR], F32, "vessel1")
@@ -243,9 +251,9 @@ def tile_list_rop_vessel_ridge_kernel(
         for t in range(PACK):
             h1.append(first_stage(1, t))
             pick_vessel(vessel1, h1[t], 1, t)
-        wb_q = [quantize(round_weight(wb_raw[:, a], on_vector, f"wb_bf{a}"), f"wb{a}") for a in range(2)]
-        xa_q = [quantize(interleave(vessel0, "scalar", "xa_bf0"), "xa0")]
-        xa_q.append(quantize(interleave(vessel1, "scalar", "xa_bf1", "gate0"), "xa1"))
+        xa_q = [quantize(interleave(vessel0, "scalar", "xa_bf0", "gate0"), "xa0")]
+        wb_bf0 = round_weight(wb_raw[:, 0], on_scalar, "wb_bf0")
+        xa_bf1 = interleave(vessel1, "scalar", "xa_bf1", "gate1")
 
         def ridge_rows(bounded, i, t0, t1, slot):
             picked = tile([P, t1 - t0, HALF], F32, f"ridge1_{i}{t0}", slot)
@@ -255,14 +263,20 @@ def tile_list_rop_vessel_ridge_kernel(
                     bound_ridge(bounded[:, t - 1, :], picked[:, t - 1 - t0, :], 1, t - 1)
             bound_ridge(bounded[:, t1 - 1, :], picked[:, t1 - 1 - t0, :], 1, t1 - 1)
 
-        xb_bf0 = interleave(ridge0_bf, "scalar", "xb_bf0", "gate1")
+        xb_bf0 = interleave(ridge0_bf, "scalar", "xb_bf0")
         bounded = [tile([P, PACK, HALF], BF16, f"ridge1_bf{i}") for i in range(2)]
         ridge_rows(bounded[0], 0, 0, PACK, "gate0")
+        wb_q = [quantize(wb_bf0, "wb0")]
+        xa_q.append(quantize(xa_bf1, "xa1"))
+        xb_bf10 = interleave(bounded[0], "scalar", "xb_bf10", "gate2")
+        ridge_rows(bounded[1], 1, 0, 2, "gate1")
         xb_q0 = quantize(xb_bf0, "xb0")
+        wb_q.append(quantize(round_weight(wb_raw[:, 1], both, "wb_bf1"), "wb1"))
+        xb_q1 = [quantize(xb_bf10, "xb1_0")]
 
         ya = tile([P, PACK, NPAIR], F32, "ya")
         for t in range(PACK):
-            bank = psum.tile([P, BANK], F32, name="bank", tag="bank")
+            bank = psum.tile([P, BANK], F32, name="ya_bank", tag="ya_bank")
             for a in range(2):
                 nc.tensor.matmul_mx(
                     out=bank[:],
@@ -275,11 +289,8 @@ def tile_list_rop_vessel_ridge_kernel(
                 )
             nc.scalar.copy(out=ya[:, t, :], in_=bank[:])
 
-        xb_bf10 = interleave(bounded[0], "scalar", "xb_bf10", "gate2")
-        ridge_rows(bounded[1], 1, 0, 2, "gate1")
-        xb_q1 = [quantize(xb_bf10, "xb1_0")]
         ridge_rows(bounded[1], 1, 2, PACK, "gate2")
-        xb_bf11 = interleave(bounded[1], "scalar", "xb_bf11")
+        xb_q1.append(quantize(interleave(bounded[1], "vector", "xb_bf11", helped=TAIL_HELP), "xb1_1"))
 
         y_codes = tile([P, NPAIR], U32, "y_codes")
         y_scales = tile([P, NPAIR], U8, "y_scales")
@@ -288,11 +299,9 @@ def tile_list_rop_vessel_ridge_kernel(
         per_bank = BANK // HALF
         for i in range(2):
             pairs = slice(i * HALF, (i + 1) * HALF)
-            if i == 1:
-                xb_q1.append(quantize(xb_bf11, "xb1_1"))
             y = tile([P, PACK, HALF], F32, f"y_{i}")
             for t0 in range(0, PACK, per_bank):
-                bank = psum.tile([P, per_bank, HALF], F32, name="bank", tag="bank")
+                bank = psum.tile([P, per_bank, HALF], F32, name="bank", tag="bank", bufs=3)
                 for a in range(2):
                     codes = xb_q0[0][:, pairs] if a == 0 else xb_q1[i][0][:]
                     scales = xb_q0[1][:, pairs] if a == 0 else xb_q1[i][1][:]
@@ -311,7 +320,7 @@ def tile_list_rop_vessel_ridge_kernel(
                     out=y[:, t0 : t0 + per_bank, :], in0=bank[:], in1=ya[:, t0 : t0 + per_bank, pairs], op=MULT
                 )
             nc.sync.dma_start(out=out_rows[:, :, pairs], in_=y[:])
-            y_bf = interleave(y, ("scalar", "vector")[i], f"y_bf{i}")
+            y_bf = interleave(y, ("scalar", "vector")[i], f"y_bf{i}", helped=i * TAIL_HELP)
             nc.vector.quantize_mx(out=y_codes[:, pairs].bitcast(FP8X4), scales=y_scales[:, pairs], in_=y_bf[:])
             nc.sync.dma_start(out=out_words[:, pairs], in_=y_codes[:, pairs].bitcast(I32))
         for q in range(4):

@@ -23,7 +23,6 @@ KP = P * PACK
 BANK = 512
 HALF = NPAIR // 2
 HEAD_SPLIT = 44
-SYNC_MOVES = 5
 TAIL_HELP = 20
 
 
@@ -96,6 +95,15 @@ def tile_list_rop_vessel_ridge_kernel(
             load_rows(raw[:], w1, a, b)
             return raw
 
+        def load_w1_halves(a, slot):
+            raw = tile([P, 2, PACK, KP // 2], F32, f"w1_raw{a}0", slot)
+            for u in range(2):
+                nc.sync.dma_start(
+                    out=raw[:, u],
+                    in_=w1[a * KP : (a + 1) * KP, u * KP // 2 : (u + 1) * KP // 2].rearrange("(p j) c -> p j c", j=PACK),
+                )
+            return raw
+
         wa_codes = tile([P, 2, 2 * N], U8, "wa_codes")
         for a in range(2):
             nc.vector.tensor_copy(
@@ -103,7 +111,7 @@ def tile_list_rop_vessel_ridge_kernel(
                 in_=wa_raw[a][:].rearrange("p (m t e) -> p m t e", t=PACK, e=2),
             )
         table.append(load_table(1, "load_c"))
-        w1_raw = {(0, 0): load_w1(0, 0, "load_a")}
+        head_raw = [load_w1_halves(0, "load_a")]
 
         wa_sc = tile([P, 2, N], U8, "wa_sc")
         nc.vector.tensor_copy(
@@ -113,8 +121,6 @@ def tile_list_rop_vessel_ridge_kernel(
 
         picked_scales = tile([P, S], U8, "picked_scales")
         nc.vector.tensor_copy(out=picked_scales[:], in_=scale_window[:].indirect(offs_t[:]))
-        v_scales = tile([P, 2, S], U8, "v_scales")
-        nc.vector.memset(v_scales[:].bitcast(I32), 0)
 
         gain_va = tile([P, 2, PACK], F32, "gain_va")
         nc.gpsimd.tensor_tensor(out=gain_va[:], in0=gain_t[:], in1=va_t[:], op=MULT)
@@ -123,25 +129,20 @@ def tile_list_rop_vessel_ridge_kernel(
             for t in range(PACK):
                 nc.scalar.copy(out=spread[:, b, t, :], in_=gain_va[:, b, t : t + 1].to_broadcast([P, NPAIR]))
 
-        for a in range(2):
+        v_scales = [tile([P, S], U8, f"v_scales{a}", ("v_scales0", "gain_va")[a]) for a in range(2)]
+        for a, queue in enumerate((nc.sync, nc.scalar)):
+            nc.gpsimd.memset(v_scales[a][:].bitcast(I32), 0)
             for q in range(4):
                 first = 64 * a + 16 * q
-                queue = nc.sync if 4 * a + q < SYNC_MOVES else nc.gpsimd
                 queue.dma_start(
-                    out=v_scales[32 * q : 32 * q + 4, a, :].bitcast(I32),
+                    out=v_scales[a][32 * q : 32 * q + 4, :].bitcast(I32),
                     in_=picked_scales[first : first + 16 : 4, :].bitcast(I32),
                 )
 
         v_codes = [tile([P, S], U32, f"v_codes{a}") for a in range(2)]
         nc.vector.tensor_copy(out=v_codes[0][:], in_=table[0][:].indirect(offs_t[:]))
-        last_raw = tile([P, 2, PACK, KP // 2], F32, "last_raw", "load_b")
-        for u in range(2):
-            nc.sync.dma_start(
-                out=last_raw[:, u],
-                in_=w1[KP : 2 * KP, u * KP // 2 : (u + 1) * KP // 2].rearrange("(p j) c -> p j c", j=PACK),
-            )
+        head_raw.append(load_w1_halves(1, "load_b"))
         nc.vector.tensor_copy(out=v_codes[1][:], in_=table[1][:].indirect(offs_t[:]))
-        w1_raw[0, 1] = load_w1(0, 1, "load_c")
 
 
         def round_weight(raw, shares, name):
@@ -169,30 +170,30 @@ def tile_list_rop_vessel_ridge_kernel(
         on_vector = (("vector", 0, P),)
         on_scalar = (("scalar", 0, P),)
         w1_q = {}
-        w1_q[0, 0] = quantize(round_weight(w1_raw[0, 0][:], both, "w1_bf00"), "w1_00", parts=2)
-        w1_raw[1, 1] = load_w1(1, 1, "load_a")
-        last_bf = tile([P, PACK * KP], BF16, "w1_bf10")
-        for u, engine in enumerate(("scalar", "vector")):
-            copy_on(
-                engine,
-                last_bf[:].rearrange("p (t m j) -> p m j t", t=PACK, j=PACK)[:, u * P // 2 : (u + 1) * P // 2],
-                last_raw[:, u].rearrange("p j (m t) -> p m j t", t=PACK),
-            )
-        w1_q[1, 0] = quantize(last_bf, "w1_10", parts=2)
+        for a in range(2):
+            rounded = tile([P, PACK * KP], BF16, f"w1_bf{a}0")
+            for u, engine in enumerate(("scalar", "vector")):
+                copy_on(
+                    engine,
+                    rounded[:].rearrange("p (t m j) -> p m j t", t=PACK, j=PACK)[:, u * P // 2 : (u + 1) * P // 2],
+                    head_raw[a][:, u].rearrange("p j (m t) -> p m j t", t=PACK),
+                )
+            w1_q[a, 0] = quantize(rounded, f"w1_{a}0", parts=2)
+        w1_raw = {(a, 1): load_w1(a, 1, ("load_a", "load_b")[a]) for a in range(2)}
 
         def first_stage(b, t):
             h = tile([P, S], F32, f"h{b}{t}")
             cols = slice(t * P, (t + 1) * P)
             for half in range(S // BANK):
                 picks = slice(half * BANK, (half + 1) * BANK)
-                bank = psum.tile([P, BANK], F32, name="bank", tag="bank", bufs=3)
+                bank = psum.tile([P, BANK], F32, name="bank", tag="bank")
                 for a in range(2):
                     nc.tensor.matmul_mx(
                         out=bank[:],
                         lhsT=w1_q[a, b][0][:, cols].bitcast(FP8X4),
                         lhsT_scale=w1_q[a, b][1][:, cols],
                         rhs=v_codes[a][:, picks].bitcast(FP8X4),
-                        rhs_scale=v_scales[:, a, picks],
+                        rhs_scale=v_scales[a][:, picks],
                         start=(a == 0),
                         stop=(a == 1),
                     )
@@ -239,7 +240,7 @@ def tile_list_rop_vessel_ridge_kernel(
         w1_q[0, 1] = quantize(round_weight(w1_raw[0, 1][:], on_scalar, "w1_bf01"), "w1_01")
         pick_both(1)
         w1_q[1, 1] = quantize(round_weight(w1_raw[1, 1][:], on_scalar, "w1_bf11"), "w1_11")
-        wb_raw = tile([P, 2, PACK, KP], F32, "wb_raw", "load_a")
+        wb_raw = tile([P, 2, PACK, KP], F32, "wb_raw", "load_b")
         for a in range(2):
             load_rows(wb_raw[:, a], wb, a, 0)
         pick_both(2)
@@ -301,7 +302,7 @@ def tile_list_rop_vessel_ridge_kernel(
             pairs = slice(i * HALF, (i + 1) * HALF)
             y = tile([P, PACK, HALF], F32, f"y_{i}")
             for t0 in range(0, PACK, per_bank):
-                bank = psum.tile([P, per_bank, HALF], F32, name="bank", tag="bank", bufs=3)
+                bank = psum.tile([P, per_bank, HALF], F32, name="bank", tag="bank")
                 for a in range(2):
                     codes = xb_q0[0][:, pairs] if a == 0 else xb_q1[i][0][:]
                     scales = xb_q0[1][:, pairs] if a == 0 else xb_q1[i][1][:]

from contextlib import ExitStack

import concourse.mybir as mybir

K, H, N, T, S, NPAIR = 1024, 1024, 512, 4096, 1024, 512
FLOPS = 2 * K * H * S + 2 * 2 * H * N * NPAIR

F32 = mybir.dt.float32
BF16 = mybir.dt.bfloat16
I32 = mybir.dt.int32
U32 = mybir.dt.uint32
U16 = mybir.dt.uint16
U8 = mybir.dt.uint8
FP8X4 = mybir.dt.float8_e4m3fn_x4
FP4X4 = mybir.dt.float4_e2m1fn_x4
MULT = mybir.AluOpType.mult
MAX = mybir.AluOpType.max
TANH = mybir.ActivationFunctionType.Tanh

P = 128
PACK = 4
KP = P * PACK
BANK = 512
HALF = NPAIR // 2
HEAD_SPLIT = 44
TAIL_HELP = 20


def tile_list_rop_vessel_ridge_kernel(
    tc, tab_words, tab_scales, offs, pos1, pos2, w1, b1, gain, va, cb, wa_words, wa_scales, wb, out_0, out_1, out_2
):
    nc = tc.nc
    with ExitStack() as ctx:
        lists = ctx.enter_context(tc.tile_pool(name="lists", bufs=1))
        sb = ctx.enter_context(tc.tile_pool(name="sb", bufs=1))
        psum = ctx.enter_context(tc.psum_pool(name="psum", bufs=4))

        def tile(shape, dtype, name, slot=None):
            return sb.tile(shape, dtype, name=name, tag=slot or name, align_bytes=64)

        def copy_on(engine, out, in_):
            if engine == "vector":
                nc.vector.tensor_copy(out=out, in_=in_)
            else:
                nc.scalar.copy(out=out, in_=in_)

        offs_t = lists.tile([P, S // 16], U16, name="offs_t")
        pos1_t = lists.tile([P, NPAIR // 16], U16, name="pos1_t")
        pos2_t = lists.tile([P, NPAIR // 16], U16, name="pos2_t")
        nc.sync.dma_start(offs_t[:], offs)

        was_raw = tile([P, 2, N], U8, "was_raw")
        nc.gpsimd.memset(was_raw[:].bitcast(I32), 0)
        for q in range(4):
            nc.scalar.dma_start(
                out=was_raw[32 * q : 32 * q + 4, :, :].bitcast(I32),
                in_=wa_scales[:, 4 * q : 4 * q + 4, :].rearrange("a r c -> r a c").bitcast(I32),
            )
        scale_window = tile([P, T], U8, "scale_window")
        nc.vector.memset(scale_window[:].bitcast(I32), 0)
        nc.scalar.dma_start(
            out=scale_window[0:P:4, :].bitcast(I32), in_=tab_scales.rearrange("a q t -> (a q) t").bitcast(I32)
        )
        nc.sync.dma_start(pos1_t[:], pos1)
        nc.sync.dma_start(pos2_t[:], pos2)

        wa_raw = [tile([P, 2 * N], U8, f"wa_raw{a}", ("load_c", "load_a")[a]) for a in range(2)]
        for a in range(2):
            nc.sync.dma_start(out=wa_raw[a][:].bitcast(I32), in_=wa_words[a].bitcast(I32))

        def load_table(a, slot):
            words = tile([P, T], U32, f"table{a}", slot)
            nc.sync.dma_start(out=words[:].bitcast(I32), in_=tab_words[a].rearrange("p t i -> p (t i)").bitcast(I32))
            return words

        table = [load_table(0, "load_b")]

        def load_vector(v, name):
            t = tile([P, 2, PACK], F32, name)
            nc.gpsimd.dma_start(out=t[:], in_=v.rearrange("(b p t) -> p b t", b=2, t=PACK))
            return t

        gain_t = load_vector(gain, "gain_t")
        va_t = load_vector(va, "va_t")
        b1_t = load_vector(b1, "b1_t")
        cb_t = load_vector(cb, "cb_t")

        def load_rows(dst, w, a, b):
            nc.sync.dma_start(
                out=dst, in_=w[a * KP : (a + 1) * KP, b * KP : (b + 1) * KP].rearrange("(p j) c -> p j c", j=PACK)
            )

        def load_w1(a, b, slot):
            raw = tile([P, PACK, KP], F32, f"w1_raw{a}{b}", slot)
            load_rows(raw[:], w1, a, b)
            return raw

        def load_w1_halves(a, slot):
            raw = tile([P, 2, PACK, KP // 2], F32, f"w1_raw{a}0", slot)
            for u in range(2):
                nc.sync.dma_start(
                    out=raw[:, u],
                    in_=w1[a * KP : (a + 1) * KP, u * KP // 2 : (u + 1) * KP // 2].rearrange("(p j) c -> p j c", j=PACK),
                )
            return raw

        wa_codes = tile([P, 2, 2 * N], U8, "wa_codes")
        for a in range(2):
            nc.vector.tensor_copy(
                out=wa_codes[:, a].rearrange("p (t m e) -> p m t e", t=PACK, e=2),
                in_=wa_raw[a][:].rearrange("p (m t e) -> p m t e", t=PACK, e=2),
            )
        table.append(load_table(1, "load_c"))
        head_raw = [load_w1_halves(0, "load_a")]

        wa_sc = tile([P, 2, N], U8, "wa_sc")
        nc.vector.tensor_copy(
            out=wa_sc[:].rearrange("p a (t m) -> p a m t", t=PACK),
            in_=was_raw[:].rearrange("p a (m t) -> p a m t", t=PACK),
        )

        picked_scales = tile([P, S], U8, "picked_scales")
        nc.vector.tensor_copy(out=picked_scales[:], in_=scale_window[:].indirect(offs_t[:]))

        gain_va = tile([P, 2, PACK], F32, "gain_va")
        nc.gpsimd.tensor_tensor(out=gain_va[:], in0=gain_t[:], in1=va_t[:], op=MULT)
        spread = tile([P, 2, PACK, NPAIR], F32, "spread")
        for b in range(2):
            for t in range(PACK):
                nc.scalar.copy(out=spread[:, b, t, :], in_=gain_va[:, b, t : t + 1].to_broadcast([P, NPAIR]))

        v_scales = [tile([P, S], U8, f"v_scales{a}", ("v_scales0", "gain_va")[a]) for a in range(2)]
        for a, queue in enumerate((nc.sync, nc.scalar)):
            nc.gpsimd.memset(v_scales[a][:].bitcast(I32), 0)
            for q in range(4):
                first = 64 * a + 16 * q
                queue.dma_start(
                    out=v_scales[a][32 * q : 32 * q + 4, :].bitcast(I32),
                    in_=picked_scales[first : first + 16 : 4, :].bitcast(I32),
                )

        v_codes = [tile([P, S], U32, f"v_codes{a}") for a in range(2)]
        nc.vector.tensor_copy(out=v_codes[0][:], in_=table[0][:].indirect(offs_t[:]))
        head_raw.append(load_w1_halves(1, "load_b"))
        nc.vector.tensor_copy(out=v_codes[1][:], in_=table[1][:].indirect(offs_t[:]))


        def round_weight(raw, shares, name):
            rounded = tile([P, PACK * KP], BF16, name)
            dst = rounded[:].rearrange("p (t m j) -> p m j t", t=PACK, j=PACK)
            src = raw.rearrange("p j (m t) -> p m j t", t=PACK)
            for engine, m0, m1 in shares:
                copy_on(engine, dst[:, m0:m1], src[:, m0:m1])
            return rounded

        def quantize(rounded, name, parts=1):
            width = rounded.shape[1] // PACK
            codes = tile([P, width], U32, name + "_codes")
            scales = tile([P, width], U8, name + "_scales")
            step = width // parts
            for c in range(0, width, step):
                nc.vector.quantize_mx(
                    out=codes[:, c : c + step].bitcast(FP8X4),
                    scales=scales[:, c : c + step],
                    in_=rounded[:, PACK * c : PACK * (c + step)],
                )
            return codes, scales

        both = (("vector", 0, HEAD_SPLIT), ("scalar", HEAD_SPLIT, P))
        on_vector = (("vector", 0, P),)
        on_scalar = (("scalar", 0, P),)
        w1_q = {}
        for a in range(2):
            rounded = tile([P, PACK * KP], BF16, f"w1_bf{a}0")
            for u, engine in enumerate(("scalar", "vector")):
                copy_on(
                    engine,
                    rounded[:].rearrange("p (t m j) -> p m j t", t=PACK, j=PACK)[:, u * P // 2 : (u + 1) * P // 2],
                    head_raw[a][:, u].rearrange("p j (m t) -> p m j t", t=PACK),
                )
            w1_q[a, 0] = quantize(rounded, f"w1_{a}0", parts=2)
        w1_raw = {(a, 1): load_w1(a, 1, ("load_a", "load_b")[a]) for a in range(2)}

        def first_stage(b, t):
            h = tile([P, S], F32, f"h{b}{t}")
            cols = slice(t * P, (t + 1) * P)
            for half in range(S // BANK):
                picks = slice(half * BANK, (half + 1) * BANK)
                bank = psum.tile([P, BANK], F32, name="bank", tag="bank")
                for a in range(2):
                    nc.tensor.matmul_mx(
                        out=bank[:],
                        lhsT=w1_q[a, b][0][:, cols].bitcast(FP8X4),
                        lhsT_scale=w1_q[a, b][1][:, cols],
                        rhs=v_codes[a][:, picks].bitcast(FP8X4),
                        rhs_scale=v_scales[a][:, picks],
                        start=(a == 0),
                        stop=(a == 1),
                    )
                nc.scalar.activation(out=h[:, picks], in_=bank[:], func=TANH, bias=b1_t[:, b, t : t + 1])
            return h

        def pick_vessel(dst, h, b, t):
            nc.vector.tensor_tensor(out=dst[:, t, :], in0=h[:].indirect(pos1_t[:]), in1=spread[:, b, t, :], op=MULT)

        def pick_ridge(dst, h, c0, c1):
            nc.vector.tensor_copy(out=dst, in_=h[:].indirect(pos2_t[:, c0 // 16 : c1 // 16]))

        def bound_ridge(dst, src, b, t):
            nc.vector.tensor_scalar(
                out=dst,
                in0=src,
                scalar1=gain_t[:, b, t : t + 1],
                scalar2=cb_t[:, b, t : t + 1],
                op0=MULT,
                op1=MAX,
            )

        def interleave(src, engine, name, slot=None, helped=0):
            woven = tile([P, PACK * src.shape[2]], BF16, name, slot)
            dst = woven[:].rearrange("p (c i t) -> p c t i", i=4, t=PACK)
            rows = src[:].rearrange("p t (c i) -> p c t i", i=4)
            copy_on(engine, dst[:, helped:], rows[:, helped:])
            if helped:
                copy_on("scalar", dst[:, :helped], rows[:, :helped])
            return woven

        vessel0 = tile([P, PACK, NPAIR], F32, "vessel0")
        ridge0 = tile([P, PACK, NPAIR], F32, "ridge0")
        ridge0_bf = tile([P, PACK, NPAIR], BF16, "ridge0_bf")

        def pick_both(t):
            h = first_stage(0, t)
            pick_vessel(vessel0, h, 0, t)
            if t > 0:
                bound_ridge(ridge0_bf[:, t - 1, :], ridge0[:, t - 1, :], 0, t - 1)
            pick_ridge(ridge0[:, t, :], h, 0, NPAIR)

        pick_both(0)
        w1_q[0, 1] = quantize(round_weight(w1_raw[0, 1][:], on_scalar, "w1_bf01"), "w1_01")
        pick_both(1)
        w1_q[1, 1] = quantize(round_weight(w1_raw[1, 1][:], on_scalar, "w1_bf11"), "w1_11")
        wb_raw = tile([P, 2, PACK, KP], F32, "wb_raw", "load_b")
        for a in range(2):
            load_rows(wb_raw[:, a], wb, a, 0)
        pick_both(2)
        pick_both(3)
        bound_ridge(ridge0_bf[:, PACK - 1, :], ridge0[:, PACK - 1, :], 0, PACK - 1)

        vessel1 = tile([P, PACK, NPAIR], F32, "vessel1")
        h1 = []
        for t in range(PACK):
            h1.append(first_stage(1, t))
            pick_vessel(vessel1, h1[t], 1, t)
        xa_q = [quantize(interleave(vessel0, "scalar", "xa_bf0", "gate0"), "xa0")]
        wb_bf0 = round_weight(wb_raw[:, 0], on_scalar, "wb_bf0")
        xa_bf1 = interleave(vessel1, "scalar", "xa_bf1", "gate1")

        def ridge_rows(bounded, i, t0, t1, slot):
            picked = tile([P, t1 - t0, HALF], F32, f"ridge1_{i}{t0}", slot)
            for t in range(t0, t1):
                pick_ridge(picked[:, t - t0, :], h1[t], i * HALF, (i + 1) * HALF)
                if t > t0:
                    bound_ridge(bounded[:, t - 1, :], picked[:, t - 1 - t0, :], 1, t - 1)
            bound_ridge(bounded[:, t1 - 1, :], picked[:, t1 - 1 - t0, :], 1, t1 - 1)

        xb_bf0 = interleave(ridge0_bf, "scalar", "xb_bf0")
        bounded = [tile([P, PACK, HALF], BF16, f"ridge1_bf{i}") for i in range(2)]
        ridge_rows(bounded[0], 0, 0, PACK, "gate0")
        wb_q = [quantize(wb_bf0, "wb0")]
        xa_q.append(quantize(xa_bf1, "xa1"))
        xb_bf10 = interleave(bounded[0], "scalar", "xb_bf10", "gate2")
        ridge_rows(bounded[1], 1, 0, 2, "gate1")
        xb_q0 = quantize(xb_bf0, "xb0")
        wb_q.append(quantize(round_weight(wb_raw[:, 1], both, "wb_bf1"), "wb1"))
        xb_q1 = [quantize(xb_bf10, "xb1_0")]

        ya = tile([P, PACK, NPAIR], F32, "ya")
        for t in range(PACK):
            bank = psum.tile([P, BANK], F32, name="ya_bank", tag="ya_bank")
            for a in range(2):
                nc.tensor.matmul_mx(
                    out=bank[:],
                    lhsT=wa_codes[:, a, 2 * t * P : 2 * (t + 1) * P].bitcast(FP4X4),
                    lhsT_scale=wa_sc[:, a, t * P : (t + 1) * P],
                    rhs=xa_q[a][0][:].bitcast(FP8X4),
                    rhs_scale=xa_q[a][1][:],
                    start=(a == 0),
                    stop=(a == 1),
                )
            nc.scalar.copy(out=ya[:, t, :], in_=bank[:])

        ridge_rows(bounded[1], 1, 2, PACK, "gate2")
        xb_q1.append(quantize(interleave(bounded[1], "vector", "xb_bf11", helped=TAIL_HELP), "xb1_1"))

        y_codes = tile([P, NPAIR], U32, "y_codes")
        y_scales = tile([P, NPAIR], U8, "y_scales")
        out_rows = out_0.rearrange("(p t) m -> p t m", t=PACK)
        out_words = out_1[0].rearrange("p m t -> p (m t)").bitcast(I32)
        per_bank = BANK // HALF
        for i in range(2):
            pairs = slice(i * HALF, (i + 1) * HALF)
            y = tile([P, PACK, HALF], F32, f"y_{i}")
            for t0 in range(0, PACK, per_bank):
                bank = psum.tile([P, per_bank, HALF], F32, name="bank", tag="bank")
                for a in range(2):
                    codes = xb_q0[0][:, pairs] if a == 0 else xb_q1[i][0][:]
                    scales = xb_q0[1][:, pairs] if a == 0 else xb_q1[i][1][:]
                    for u in range(per_bank):
                        cols = slice((t0 + u) * P, (t0 + u + 1) * P)
                        nc.tensor.matmul_mx(
                            out=bank[:, u, :],
                            lhsT=wb_q[a][0][:, cols].bitcast(FP8X4),
                            lhsT_scale=wb_q[a][1][:, cols],
                            rhs=codes.bitcast(FP8X4),
                            rhs_scale=scales,
                            start=(a == 0 and u == 0),
                            stop=(a == 1 and u == per_bank - 1),
                        )
                nc.vector.tensor_tensor(
                    out=y[:, t0 : t0 + per_bank, :], in0=bank[:], in1=ya[:, t0 : t0 + per_bank, pairs], op=MULT
                )
            nc.sync.dma_start(out=out_rows[:, :, pairs], in_=y[:])
            y_bf = interleave(y, ("scalar", "vector")[i], f"y_bf{i}", helped=i * TAIL_HELP)
            nc.vector.quantize_mx(out=y_codes[:, pairs].bitcast(FP8X4), scales=y_scales[:, pairs], in_=y_bf[:])
            nc.sync.dma_start(out=out_words[:, pairs], in_=y_codes[:, pairs].bitcast(I32))
        for q in range(4):
            queue = nc.sync if q % 2 == 0 else nc.scalar
            queue.dma_start(
                out=out_2[0, 4 * q : 4 * q + 4, :].bitcast(I32), in_=y_scales[32 * q : 32 * q + 4, :].bitcast(I32)
            )
